import numpy as np, ml_dtypes
CORES = [50,106,114,52,108,116]
N = 6
import mx_ref
NC = 128
BF = ml_dtypes.bfloat16
def cut(t, i, w=512):
    return t[:, w * i:w * i + w]
def term(a, B):
    return np.stack([mx_ref.matmul(mx_ref.quantize(cut(a, i)), B) for i in range(4)], axis=2).reshape(128, -1)
def setup_inputs(rng):
    def f(*shape):
        return mx_ref.flush((rng.standard_normal(shape, dtype=np.float32) * np.exp2(rng.integers(-2, 3, shape[:-1] + (1,)))).astype(BF))
    return {"a": f(N, 128, 4 * 512), "b": f(N, 128, N * 4 * NC)}
def setup_inputs_blocks(rng):
    d = setup_inputs(rng)
    for k in ("a", "b"): d[k] = mx_ref.spread(d[k], rng, 2)
    return d
def setup_inputs_wide(rng):
    d = setup_inputs(rng)
    for k in ("a", "b"): d[k] = mx_ref.flush((d[k].astype(np.float32) * np.exp2(rng.integers(-4, 5, (N, 1, 1))).astype(np.float32)).astype(BF))
    return d
def setup_inputs_lossless(rng):
    a = np.zeros((N, 128, 4 * 128, 4), np.float32)
    for r in range(N):
        k = rng.integers(0, 512, size=4 * 128)
        a[r, k // 4, np.arange(4 * 128), k % 4] = 1.0
    size = np.repeat(2.0 ** rng.integers(-4, 5, size=(1, 1, (N * 4 * NC) // 4)), 4, axis=2)
    b = rng.integers(-1, 2, size=(N, 128, N * 4 * NC)) * size
    return {"a": a.reshape(N, 128, 4 * 512).astype(BF), "b": b.astype(np.float32).astype(BF)}
def reference(a, b):
    y = np.zeros((N, 128, 4 * NC), np.float32)
    for c in range(N):
        y[c] = mx_ref.total([term(a[r], mx_ref.quantize(cut(b[r], c, 4 * NC))) for r in range(N)])
    return {"y": y}

@@ -1,0 +1,279 @@
+from concourse.bass import DstId, RemoteDMATransfer
+from concourse.mybir import dt, AluOpType, ActivationFunctionType
+
+W = 128
+TW = 4 * W
+NSIM = 128
+EW = TW + 4
+A_PARTS = 2
+X4 = "float8_e4m3fn_x4"
+
+SCRATCH = {
+    "a_sb": ("sbuf", [128, 4 * TW], "bfloat16"),
+    "b_sb": ("sbuf", [128, 6 * TW], "bfloat16"),
+    "aq": ("sbuf", [128, 4 * W], X4), "asc": ("sbuf", [128, 4 * W], "uint8"),
+    "bq": ("sbuf", [128, 6 * W], X4), "bsc": ("sbuf", [128, 6 * W], "uint8"),
+    "e_sb": ("sbuf", [128, EW], "bfloat16"),
+    "sq": ("sbuf", [128, 4 * W], X4), "ssc": ("sbuf", [128, 4 * W], "uint8"),
+    "hA": ("sbuf", [128, 2 * TW], "bfloat16"), "hAq": ("sbuf", [128, 2 * W], X4), "hAs": ("sbuf", [128, 2 * W], "uint8"),
+    "hB": ("sbuf", [128, 2 * TW], "bfloat16"), "hBq": ("sbuf", [128, 2 * W], X4), "hBs": ("sbuf", [128, 2 * W], "uint8"),
+    "hP": ("sbuf", [128, TW], "bfloat16"), "hPq": ("sbuf", [128, W], X4), "hPs": ("sbuf", [128, W], "uint8"),
+    "lS0q": ("sbuf", [128, 2 * W], X4), "lS0s": ("sbuf", [128, 2 * W], "uint8"),
+    "lS1q": ("sbuf", [128, 2 * W], X4), "lS1s": ("sbuf", [128, 2 * W], "uint8"),
+    "lPq": ("sbuf", [128, W], X4), "lPs": ("sbuf", [128, W], "uint8"),
+    "lX0q": ("sbuf", [128, W], X4), "lX0s": ("sbuf", [128, W], "uint8"),
+    "lX1q": ("sbuf", [128, W], X4), "lX1s": ("sbuf", [128, W], "uint8"),
+    "ysb": ("sbuf", [128, TW], "float32"),
+    "ps0": ("psum", [128, 4 * 512], "float32"),
+    "ps1": ("psum", [128, 4 * 512], "float32"),
+}
+SEMAPHORES = (["c1", "c2", "sel", "ev0", "ev1", "hqA", "hqB", "hqP", "s0", "s1", "pa", "x0", "x1", "sent", "yev", "st"]
+              + ["ld%d" % k for k in range(10)] + ["aq%d" % i for i in range(4)] + ["bq%d" % k for k in range(6)]
+              + ["m0%d" % i for i in range(4)] + ["m1%d" % i for i in range(4)])
+
+
+def _plan(cores, topo):
+    plan = {}
+    for c0 in cores:
+        X = topo.chip(c0)
+        if X in plan:
+            continue
+        mine = [c for c in cores if topo.chip(c) == X]
+        off = [r for r in range(len(cores)) if topo.chip(cores[r]) != X]
+        share = len(off) // 2
+        left, js, able = list(off), [], []
+        for c in mine:
+            can = [r for r in off if topo.may_write(c, cores[r])]
+            if len(can) == len(off):
+                able.append(c)
+            elif len(can) >= share:
+                take = [r for r in can if r in left][:share]
+                js.append((c, take))
+                left = [r for r in left if r not in take]
+        need = len(left) // share
+        summers = able[:need]
+        for c in range(NSIM):
+            if len(summers) >= need:
+                break
+            if (topo.chip(c) == X and c not in cores and all(topo.may_write(c, cores[r]) for r in left)
+                    and all(topo.die(c) != topo.die(s) for s in summers)):
+                summers.append(c)
+        if need == 1:
+            js.append((summers[0], left))
+        elif need == 2:
+            near = [r for r in left if topo.die(cores[r]) == topo.die(summers[0])]
+            if len(near) != share:
+                near = left[:share]
+            js.append((summers[0], near))
+            js.append((summers[1], [r for r in left if r not in near]))
+        helped = any(j[0] not in cores for j in js)
+        js = [(j[0], j[1], (2 if j[0] not in cores else 1) if helped else 0) for j in js]
+        plan[X] = sorted(js, key=lambda j: -j[2])
+    return plan
+
+
+def _runs(ts):
+    out = []
+    for t in sorted(ts):
+        if out and out[-1][-1] == t - 1:
+            out[-1].append(t)
+        else:
+            out.append([t])
+    return out
+
+
+def rank_program(g, core, T, topo):
+    cores = [int(c) for c in T.cores]
+    plan = _plan(cores, topo)
+    X = topo.chip(core)
+    if X not in plan:
+        return
+    jobs = plan[X]
+    rank = T.rank_of(core)
+    kept = ([j for j in jobs if j[0] == core] + [None])[0]
+    if rank is None and kept is None:
+        return
+    S = T.sem
+    u8 = dt.uint8
+    mine = [r for r in range(len(cores)) if topo.chip(cores[r]) == X]
+    sent = [0]
+
+    def bits(src, dst):
+        m = topo.mask(src, dst)
+        return [e for e in range(m.bit_length()) if (m >> e) & 1]
+
+    def to_mask(es):
+        return sum(1 << e for e in es)
+
+    def sources(d):
+        out = [j for Y in plan for j in plan[Y] if d in j[1]]
+        return sorted(out, key=lambda j: j[2])
+
+    def send(dst, name, land, sem, ncol):
+        rid, pid, _se = topo.addr(dst)
+        es = bits(core, dst)
+        g.remote_dma(T[land + "q"][:, 0:ncol].bitcast(u8), T[name + "q"][:, 0:ncol].bitcast(u8), sem, S.sent,
+                     pid, rid, to_mask(es))
+        g.remote_dma(T[land + "s"][:, 0:ncol], T[name + "s"][:, 0:ncol], sem, S.sent, pid, rid, to_mask(es))
+        sent[0] += 2 * len(es)
+
+    def evac(ps, ncol, mm, cnt, out_of, done, who):
+        for i in range(4):
+            src = ps[:, 512 * i:512 * i + ncol]
+            if who[i] == "v":
+                g.vector.wait_ge(S[mm % i], cnt)
+                g.vector.tensor_copy(out_of(i), src).then_inc(done, 1)
+            else:
+                g.scalar.wait_ge(S[mm % i], cnt)
+                g.scalar.activation(out_of(i), src, ActivationFunctionType.Copy).then_inc(done, 1)
+
+    def pack(name, ncol, ev, cnt, done):
+        g.vector.wait_ge(ev, cnt)
+        g.vector.quantize_mx(T[name + "q"][:, 0:ncol], T[name + "s"][:, 0:ncol], T[name][:, 0:4 * ncol]).then_inc(done, 1)
+
+    def pick(i):
+        return T.sq[:, W * i:W * i + W], T.ssc[:, W * i:W * i + W]
+
+    def sum_stage(fresh):
+        nd = len(kept[1])
+        senders = [r for r in mine if cores[r] != core]
+        g.tensor.wait_ge(S.sel, 4)
+        for k, r in enumerate(senders):
+            slot = mine.index(r)
+            g.tensor.wait_ge(S["s%d" % slot], 2 * len(bits(cores[r], core)))
+            last = k == len(senders) - 1
+            for i in range(4):
+                sq, ss = pick(i)
+                ins = g.tensor.matmul_mx(T.ps1[:, 512 * i:512 * i + nd * W], sq, ss, T["lS%dq" % slot][:, 0:nd * W],
+                                         T["lS%ds" % slot][:, 0:nd * W], fresh and k == 0, last)
+                if last:
+                    ins.then_inc(S["m1%d" % i], 1)
+        evac(T.ps1, nd * W, "m1%d", 1, lambda i: T.hB[:, i:4 * nd * W:4], S.ev1, "vsvs")
+        pack("hB", nd * W, S.ev1, 4, S.hqB)
+        g.wait_ge(S.hqB, 1)
+        for part in ("q", "s"):
+            trs = []
+            for k, d in enumerate(kept[1]):
+                rid, pid, _se = topo.addr(cores[d])
+                es = bits(core, cores[d])
+                es = es[k * (len(es) // nd):(k + 1) * (len(es) // nd)]
+                slot = sources(d).index(kept)
+                src, dst = T["hB" + part][:, W * k:W * k + W], T["lX%d%s" % (slot, part)][:, 0:W]
+                if part == "q":
+                    src, dst = src.bitcast(u8), dst.bitcast(u8)
+                trs.append(RemoteDMATransfer(dst_ids=[DstId(rid=rid, pnc=pid)], dma_engine_mask=to_mask(es),
+                                             remote_sem=S["x%d" % slot], src=src, dst=dst))
+                sent[0] += len(es)
+            g.remote_dma_fused(trs, local_sem=S.sent)
+
+    if rank is not None:
+        partner = [r for r in mine if r != rank][0]
+        road = [j for j in jobs if j[0] != core] + ([kept] if kept else [])
+        order = road[0][1] + road[1][1] + [partner, rank]
+        pos = {t: k for k, t in enumerate(order)}
+        loads, ld_b, ld_a = [], {}, {}
+        for r in _runs(road[0][1]):
+            for t in r:
+                ld_b[t] = len(loads)
+            loads.append((T.b_sb, T.b, TW * r[0], TW * (r[-1] + 1)))
+        per = 4 // A_PARTS
+        for h in range(A_PARTS):
+            for i in range(per * h, per * h + per):
+                ld_a[i] = len(loads)
+            loads.append((T.a_sb, T.a, TW * per * h, TW * per * (h + 1)))
+        rest = sorted(_runs([t for t in order if t not in road[0][1]]), key=lambda r: min(pos[t] for t in r))
+        for r in rest:
+            for t in r:
+                ld_b[t] = len(loads)
+            loads.append((T.b_sb, T.b, TW * r[0], TW * (r[-1] + 1)))
+        for k, (buf, src, c0, c1) in enumerate(loads):
+            q = g.sync if k % 2 == 0 else g.scalar
+            q.dma_start(buf[:, c0:c1], src[:, c0:c1]).then_inc(S["ld%d" % k], 16)
+
+    g.vector.memset(T.e_sb[:], 1.0).then_inc(S.c1, 1)
+    g.wait_ge(S.c1, 1)
+    g.affine_select(T.e_sb[:], T.e_sb[:], [[-1, EW]], AluOpType.is_equal, 0.0, 3, 4).then_inc(S.c2, 1)
+    g.vector.wait_ge(S.c2, 1)
+    for i in range(4):
+        sq, ss = pick(i)
+        g.vector.quantize_mx(sq, ss, T.e_sb[:, 3 - i:3 - i + TW]).then_inc(S.sel, 1)
+
+    if rank is None:
+        sum_stage(True)
+        g.wait_ge(S.sent, sent[0])
+        return
+
+    def quant_b(t):
+        k = pos[t]
+        g.vector.wait_ge(S["ld%d" % ld_b[t]], 16)
+        g.vector.quantize_mx(T.bq[:, W * k:W * k + W], T.bsc[:, W * k:W * k + W],
+                             T.b_sb[:, TW * t:TW * t + TW]).then_inc(S["bq%d" % k], 1)
+
+    def products(ps, tiles, mm, stop, first=False):
+        k0, nc = pos[tiles[0]], W * len(tiles)
+        for t in tiles:
+            g.tensor.wait_ge(S["bq%d" % pos[t]], 1)
+        for i in range(4):
+            if first:
+                g.tensor.wait_ge(S["aq%d" % i], 1)
+            ins = g.tensor.matmul_mx(ps[:, 512 * i:512 * i + nc], T.aq[:, W * i:W * i + W], T.asc[:, W * i:W * i + W],
+                                     T.bq[:, W * k0:W * k0 + nc], T.bsc[:, W * k0:W * k0 + nc], True, stop)
+            if stop:
+                ins.then_inc(S[mm % i], 1)
+
+    my_slot = mine.index(rank)
+    for t in road[0][1]:
+        quant_b(t)
+    for i in range(4):
+        g.vector.wait_ge(S["ld%d" % ld_a[i]], 16)
+        g.vector.quantize_mx(T.aq[:, W * i:W * i + W], T.asc[:, W * i:W * i + W],
+                             T.a_sb[:, TW * i:TW * i + TW]).then_inc(S["aq%d" % i], 1)
+    n0 = len(road[0][1])
+    products(T.ps0, road[0][1], "m0%d", True, first=True)
+    evac(T.ps0, n0 * W, "m0%d", 1, lambda i: T.hA[:, i:4 * n0 * W:4], S.ev0, "sssv")
+    pack("hA", n0 * W, S.ev0, 4, S.hqA)
+    g.wait_ge(S.hqA, 1)
+    send(road[0][0], "hA", "lS%d" % my_slot, S["s%d" % my_slot], n0 * W)
+
+    for t in sorted([t for t in order if t not in road[0][1]], key=lambda t: (ld_b[t], pos[t])):
+        quant_b(t)
+
+    n1 = len(road[1][1])
+    products(T.ps1, road[1][1], "m1%d", kept is None)
+    if kept is None:
+        evac(T.ps1, n1 * W, "m1%d", 1, lambda i: T.hB[:, i:4 * n1 * W:4], S.ev1, "vsvs")
+        pack("hB", n1 * W, S.ev1, 4, S.hqB)
+        g.wait_ge(S.hqB, 1)
+        send(road[1][0], "hB", "lS%d" % my_slot, S["s%d" % my_slot], n1 * W)
+
+    g.tensor.wait_ge(S.ev0, 4)
+    products(T.ps0, [partner], "m0%d", True)
+    evac(T.ps0, W, "m0%d", 2, lambda i: T.hP[:, i:TW:4], S.ev0, "vsvs")
+    pack("hP", W, S.ev0, 8, S.hqP)
+    g.wait_ge(S.hqP, 1)
+    send(cores[partner], "hP", "lP", S.pa, W)
+
+    if kept is not None:
+        sum_stage(False)
+
+    g.tensor.wait_ge(S.ev0, 8)
+    products(T.ps0, [rank], "m0%d", False)
+    g.tensor.wait_ge(S.sel, 4)
+    srcs = sources(rank)
+    arrivals = [("lP", S.pa, 2 * len(bits(cores[partner], core)))]
+    for k, j in enumerate(srcs):
+        arrivals.append(("lX%d" % k, S["x%d" % k], 2 * (len(bits(j[0], core)) // len(j[1]))))
+    for k, (land, sem, cnt) in enumerate(arrivals):
+        g.tensor.wait_ge(sem, cnt)
+        last = k == len(arrivals) - 1
+        for i in range(4):
+            sq, ss = pick(i)
+            ins = g.tensor.matmul_mx(T.ps0[:, 512 * i:512 * i + W], sq, ss, T[land + "q"][:, 0:W], T[land + "s"][:, 0:W],
+                                     False, last)
+            if last:
+                ins.then_inc(S["m0%d" % i], 1)
+    evac(T.ps0, W, "m0%d", 3, lambda i: T.ysb[:, i:TW:4], S.yev, "vsvs")
+    g.sync.wait_ge(S.yev, 4)
+    g.sync.dma_start(T.y[:], T.ysb[:]).then_inc(S.st, 16)
+    g.sync.wait_ge(S.st, 16)
+    g.wait_ge(S.sent, sent[0])

@@ -18,18 +18,27 @@ SCRATCH = {
     "hA": ("sbuf", [128, 2 * TW], "bfloat16"), "hAq": ("sbuf", [128, 2 * W], X4), "hAs": ("sbuf", [128, 2 * W], "uint8"),
     "hB": ("sbuf", [128, 2 * TW], "bfloat16"), "hBq": ("sbuf", [128, 2 * W], X4), "hBs": ("sbuf", [128, 2 * W], "uint8"),
     "hP": ("sbuf", [128, TW], "bfloat16"), "hPq": ("sbuf", [128, W], X4), "hPs": ("sbuf", [128, W], "uint8"),
-    "lS0q": ("sbuf", [128, 2 * W], X4), "lS0s": ("sbuf", [128, 2 * W], "uint8"),
-    "lS1q": ("sbuf", [128, 2 * W], X4), "lS1s": ("sbuf", [128, 2 * W], "uint8"),
+    "lSq": ("sbuf", [128, 2 * W], X4), "lSs": ("sbuf", [128, 2 * W], "uint8"),
     "lPq": ("sbuf", [128, W], X4), "lPs": ("sbuf", [128, W], "uint8"),
     "lX0q": ("sbuf", [128, W], X4), "lX0s": ("sbuf", [128, W], "uint8"),
     "lX1q": ("sbuf", [128, W], X4), "lX1s": ("sbuf", [128, W], "uint8"),
+    "lX2q": ("sbuf", [128, W], X4), "lX2s": ("sbuf", [128, W], "uint8"),
     "ysb": ("sbuf", [128, TW], "float32"),
     "ps0": ("psum", [128, 4 * 512], "float32"),
     "ps1": ("psum", [128, 4 * 512], "float32"),
 }
-SEMAPHORES = (["c1", "c2", "sel", "ev0", "ev1", "hqA", "hqB", "hqP", "s0", "s1", "pa", "x0", "x1", "sent", "yev", "st"]
+SEMAPHORES = (["c1", "c2", "sel", "ev0", "ev1", "hqA", "hqB", "hqP", "sq", "ss", "pa", "x0", "x1", "x2", "sent", "yev",
+               "st"]
               + ["ld%d" % k for k in range(10)] + ["aq%d" % i for i in range(4)] + ["bq%d" % k for k in range(6)]
               + ["m0%d" % i for i in range(4)] + ["m1%d" % i for i in range(4)])
+
+
+def _outside(cores, topo, X, dests, dies):
+    for c in range(NSIM):
+        if (topo.chip(c) == X and c not in cores and topo.die(c) not in dies
+                and all(topo.may_write(c, cores[r]) for r in dests)):
+            return c
+    return None
 
 
 def _plan(cores, topo):
@@ -41,34 +50,38 @@ def _plan(cores, topo):
         mine = [c for c in cores if topo.chip(c) == X]
         off = [r for r in range(len(cores)) if topo.chip(cores[r]) != X]
         share = len(off) // 2
-        left, js, able = list(off), [], []
+        left, roads, able = list(off), [], []
         for c in mine:
             can = [r for r in off if topo.may_write(c, cores[r])]
             if len(can) == len(off):
                 able.append(c)
             elif len(can) >= share:
                 take = [r for r in can if r in left][:share]
-                js.append((c, take))
+                roads.append(("sum", c, take))
                 left = [r for r in left if r not in take]
         need = len(left) // share
-        summers = able[:need]
-        for c in range(NSIM):
-            if len(summers) >= need:
-                break
-            if (topo.chip(c) == X and c not in cores and all(topo.may_write(c, cores[r]) for r in left)
-                    and all(topo.die(c) != topo.die(s) for s in summers)):
-                summers.append(c)
+        heads = able[:need]
+        if len(heads) < need:
+            heads.append(_outside(cores, topo, X, left, [topo.die(s) for s in heads]))
         if need == 1:
-            js.append((summers[0], left))
+            roads.append(("sum", heads[0], left))
         elif need == 2:
-            near = [r for r in left if topo.die(cores[r]) == topo.die(summers[0])]
+            near = [r for r in left if topo.die(cores[r]) == topo.die(heads[0])]
             if len(near) != share:
                 near = left[:share]
-            js.append((summers[0], near))
-            js.append((summers[1], [r for r in left if r not in near]))
-        helped = any(j[0] not in cores for j in js)
-        js = [(j[0], j[1], (2 if j[0] not in cores else 1) if helped else 0) for j in js]
-        plan[X] = sorted(js, key=lambda j: -j[2])
+            for s, ds in ((heads[0], near), (heads[1], [r for r in left if r not in near])):
+                roads.append(("sum" if s in cores else "relay", s, ds))
+        plan[X] = roads
+    for Z in plan:
+        dies = []
+        for X in plan:
+            for k, road in enumerate(plan[X]):
+                if road[0] == "sum" and all(topo.chip(cores[d]) == Z for d in road[2]):
+                    if topo.die(road[1]) in dies:
+                        h = _outside(cores, topo, X, road[2], dies)
+                        if h is not None:
+                            plan[X][k] = ("relay", h, road[2])
+                    dies.append(topo.die(plan[X][k][1]))
     return plan
 
 
@@ -88,10 +101,9 @@ def rank_program(g, core, T, topo):
     X = topo.chip(core)
     if X not in plan:
         return
-    jobs = plan[X]
     rank = T.rank_of(core)
-    kept = ([j for j in jobs if j[0] == core] + [None])[0]
-    if rank is None and kept is None:
+    headed = ([j for j in plan[X] if j[1] == core] + [None])[0]
+    if rank is None and headed is None:
         return
     S = T.sem
     u8 = dt.uint8
@@ -105,17 +117,53 @@ def rank_program(g, core, T, topo):
     def to_mask(es):
         return sum(1 << e for e in es)
 
-    def sources(d):
-        out = [j for Y in plan for j in plan[Y] if d in j[1]]
-        return sorted(out, key=lambda j: j[2])
+    def part_of(c, road):
+        if road[0] == "sum":
+            return ("keep", 3) if road[1] == c else ("feed", 0)
+        return ("direct", 1) if all(topo.may_write(c, cores[d]) for d in road[2]) else ("feed", 2)
 
-    def send(dst, name, land, sem, ncol):
+    def sources(d):
+        out = []
+        for Y in plan:
+            for road in plan[Y]:
+                if d in road[2]:
+                    out.append((1 if road[0] == "sum" else 2, road[1], len(road[2])))
+                    if road[0] == "relay":
+                        out += [(0, c, len(road[2])) for c in cores
+                                if topo.chip(c) == Y and part_of(c, road)[0] == "direct"]
+        return [(s[1], s[2]) for s in sorted(out, key=lambda s: s[0])]
+
+    def send(dst, name, land, semq, sems, ncol):
         rid, pid, _se = topo.addr(dst)
         es = bits(core, dst)
-        g.remote_dma(T[land + "q"][:, 0:ncol].bitcast(u8), T[name + "q"][:, 0:ncol].bitcast(u8), sem, S.sent,
+        g.remote_dma(T[land + "q"][:, 0:ncol].bitcast(u8), T[name + "q"][:, 0:ncol].bitcast(u8), semq, S.sent,
                      pid, rid, to_mask(es))
-        g.remote_dma(T[land + "s"][:, 0:ncol], T[name + "s"][:, 0:ncol], sem, S.sent, pid, rid, to_mask(es))
+        g.remote_dma(T[land + "s"][:, 0:ncol], T[name + "s"][:, 0:ncol], sems, S.sent, pid, rid, to_mask(es))
         sent[0] += 2 * len(es)
+
+    def scatter(name, dests, part):
+        nd, trs = len(dests), []
+        for k, d in enumerate(dests):
+            rid, pid, _se = topo.addr(cores[d])
+            es = bits(core, cores[d])
+            es = es[k * (len(es) // nd):(k + 1) * (len(es) // nd)]
+            slot = [s[0] for s in sources(d)].index(core)
+            src, dst = T[name + part][:, W * k:W * k + W], T["lX%d%s" % (slot, part)][:, 0:W]
+            if part == "q":
+                src, dst = src.bitcast(u8), dst.bitcast(u8)
+            trs.append(RemoteDMATransfer(dst_ids=[DstId(rid=rid, pnc=pid)], dma_engine_mask=to_mask(es),
+                                         remote_sem=S["x%d" % slot], src=src, dst=dst))
+            sent[0] += len(es)
+        g.remote_dma_fused(trs, local_sem=S.sent)
+
+    if rank is None:
+        feeder = [cores[r] for r in mine if part_of(cores[r], headed)[0] == "feed"][0]
+        g.wait_ge(S.sq, len(bits(feeder, core)))
+        scatter("lS", headed[2], "q")
+        g.wait_ge(S.ss, len(bits(feeder, core)))
+        scatter("lS", headed[2], "s")
+        g.wait_ge(S.sent, sent[0])
+        return
 
     def evac(ps, ncol, mm, cnt, out_of, done, who):
         for i in range(4):
@@ -130,65 +178,40 @@ def rank_program(g, core, T, topo):
     def pack(name, ncol, ev, cnt, done):
         g.vector.wait_ge(ev, cnt)
         g.vector.quantize_mx(T[name + "q"][:, 0:ncol], T[name + "s"][:, 0:ncol], T[name][:, 0:4 * ncol]).then_inc(done, 1)
+        g.wait_ge(done, 1)
 
     def pick(i):
         return T.sq[:, W * i:W * i + W], T.ssc[:, W * i:W * i + W]
 
-    def sum_stage(fresh):
-        nd = len(kept[1])
-        senders = [r for r in mine if cores[r] != core]
-        g.tensor.wait_ge(S.sel, 4)
-        for k, r in enumerate(senders):
-            slot = mine.index(r)
-            g.tensor.wait_ge(S["s%d" % slot], 2 * len(bits(cores[r], core)))
-            last = k == len(senders) - 1
-            for i in range(4):
-                sq, ss = pick(i)
-                ins = g.tensor.matmul_mx(T.ps1[:, 512 * i:512 * i + nd * W], sq, ss, T["lS%dq" % slot][:, 0:nd * W],
-                                         T["lS%ds" % slot][:, 0:nd * W], fresh and k == 0, last)
-                if last:
-                    ins.then_inc(S["m1%d" % i], 1)
-        evac(T.ps1, nd * W, "m1%d", 1, lambda i: T.hB[:, i:4 * nd * W:4], S.ev1, "vsvs")
-        pack("hB", nd * W, S.ev1, 4, S.hqB)
-        g.wait_ge(S.hqB, 1)
-        for part in ("q", "s"):
-            trs = []
-            for k, d in enumerate(kept[1]):
-                rid, pid, _se = topo.addr(cores[d])
-                es = bits(core, cores[d])
-                es = es[k * (len(es) // nd):(k + 1) * (len(es) // nd)]
-                slot = sources(d).index(kept)
-                src, dst = T["hB" + part][:, W * k:W * k + W], T["lX%d%s" % (slot, part)][:, 0:W]
-                if part == "q":
-                    src, dst = src.bitcast(u8), dst.bitcast(u8)
-                trs.append(RemoteDMATransfer(dst_ids=[DstId(rid=rid, pnc=pid)], dma_engine_mask=to_mask(es),
-                                             remote_sem=S["x%d" % slot], src=src, dst=dst))
-                sent[0] += len(es)
-            g.remote_dma_fused(trs, local_sem=S.sent)
+    def leave(road, name):
+        if part_of(core, road)[0] == "feed":
+            send(road[1], name, "lS", S.sq, S.ss, W * len(road[2]))
+        else:
+            scatter(name, road[2], "q")
+            scatter(name, road[2], "s")
 
-    if rank is not None:
-        partner = [r for r in mine if r != rank][0]
-        road = [j for j in jobs if j[0] != core] + ([kept] if kept else [])
-        order = road[0][1] + road[1][1] + [partner, rank]
-        pos = {t: k for k, t in enumerate(order)}
-        loads, ld_b, ld_a = [], {}, {}
-        for r in _runs(road[0][1]):
-            for t in r:
-                ld_b[t] = len(loads)
-            loads.append((T.b_sb, T.b, TW * r[0], TW * (r[-1] + 1)))
-        per = 4 // A_PARTS
-        for h in range(A_PARTS):
-            for i in range(per * h, per * h + per):
-                ld_a[i] = len(loads)
-            loads.append((T.a_sb, T.a, TW * per * h, TW * per * (h + 1)))
-        rest = sorted(_runs([t for t in order if t not in road[0][1]]), key=lambda r: min(pos[t] for t in r))
-        for r in rest:
-            for t in r:
-                ld_b[t] = len(loads)
-            loads.append((T.b_sb, T.b, TW * r[0], TW * (r[-1] + 1)))
-        for k, (buf, src, c0, c1) in enumerate(loads):
-            q = g.sync if k % 2 == 0 else g.scalar
-            q.dma_start(buf[:, c0:c1], src[:, c0:c1]).then_inc(S["ld%d" % k], 16)
+    partner = [r for r in mine if r != rank][0]
+    road = sorted(plan[X], key=lambda j: part_of(core, j)[1])
+    keeps = part_of(core, road[1])[0] == "keep"
+    order = road[0][2] + road[1][2] + [partner, rank]
+    pos = {t: k for k, t in enumerate(order)}
+    loads, ld_b, ld_a = [], {}, {}
+    for r in _runs(road[0][2]):
+        for t in r:
+            ld_b[t] = len(loads)
+        loads.append((T.b_sb, T.b, TW * r[0], TW * (r[-1] + 1)))
+    per = 4 // A_PARTS
+    for h in range(A_PARTS):
+        for i in range(per * h, per * h + per):
+            ld_a[i] = len(loads)
+        loads.append((T.a_sb, T.a, TW * per * h, TW * per * (h + 1)))
+    for r in sorted(_runs([t for t in order if t not in road[0][2]]), key=lambda r: min(pos[t] for t in r)):
+        for t in r:
+            ld_b[t] = len(loads)
+        loads.append((T.b_sb, T.b, TW * r[0], TW * (r[-1] + 1)))
+    for k, (buf, src, c0, c1) in enumerate(loads):
+        q = g.sync if k % 2 == 0 else g.scalar
+        q.dma_start(buf[:, c0:c1], src[:, c0:c1]).then_inc(S["ld%d" % k], 16)
 
     g.vector.memset(T.e_sb[:], 1.0).then_inc(S.c1, 1)
     g.wait_ge(S.c1, 1)
@@ -197,11 +220,6 @@ def rank_program(g, core, T, topo):
     for i in range(4):
         sq, ss = pick(i)
         g.vector.quantize_mx(sq, ss, T.e_sb[:, 3 - i:3 - i + TW]).then_inc(S.sel, 1)
-
-    if rank is None:
-        sum_stage(True)
-        g.wait_ge(S.sent, sent[0])
-        return
 
     def quant_b(t):
         k = pos[t]
@@ -221,57 +239,59 @@ def rank_program(g, core, T, topo):
             if stop:
                 ins.then_inc(S[mm % i], 1)
 
-    my_slot = mine.index(rank)
-    for t in road[0][1]:
+    def unpack(ps, nc, land, last, mm):
+        for i in range(4):
+            sq, ss = pick(i)
+            ins = g.tensor.matmul_mx(ps[:, 512 * i:512 * i + nc], sq, ss, T[land + "q"][:, 0:nc], T[land + "s"][:, 0:nc],
+                                     False, last)
+            if last:
+                ins.then_inc(S[mm % i], 1)
+
+    for t in road[0][2]:
         quant_b(t)
     for i in range(4):
         g.vector.wait_ge(S["ld%d" % ld_a[i]], 16)
         g.vector.quantize_mx(T.aq[:, W * i:W * i + W], T.asc[:, W * i:W * i + W],
                              T.a_sb[:, TW * i:TW * i + TW]).then_inc(S["aq%d" % i], 1)
-    n0 = len(road[0][1])
-    products(T.ps0, road[0][1], "m0%d", True, first=True)
-    evac(T.ps0, n0 * W, "m0%d", 1, lambda i: T.hA[:, i:4 * n0 * W:4], S.ev0, "sssv")
-    pack("hA", n0 * W, S.ev0, 4, S.hqA)
-    g.wait_ge(S.hqA, 1)
-    send(road[0][0], "hA", "lS%d" % my_slot, S["s%d" % my_slot], n0 * W)
+    n0, n1 = W * len(road[0][2]), W * len(road[1][2])
+    products(T.ps0, road[0][2], "m0%d", True, first=True)
+    evac(T.ps0, n0, "m0%d", 1, lambda i: T.hA[:, i:4 * n0:4], S.ev0, "sssv")
+    pack("hA", n0, S.ev0, 4, S.hqA)
+    leave(road[0], "hA")
 
-    for t in sorted([t for t in order if t not in road[0][1]], key=lambda t: (ld_b[t], pos[t])):
+    for t in sorted([t for t in order if t not in road[0][2]], key=lambda t: (ld_b[t], pos[t])):
         quant_b(t)
 
-    n1 = len(road[1][1])
-    products(T.ps1, road[1][1], "m1%d", kept is None)
-    if kept is None:
-        evac(T.ps1, n1 * W, "m1%d", 1, lambda i: T.hB[:, i:4 * n1 * W:4], S.ev1, "vsvs")
-        pack("hB", n1 * W, S.ev1, 4, S.hqB)
-        g.wait_ge(S.hqB, 1)
-        send(road[1][0], "hB", "lS%d" % my_slot, S["s%d" % my_slot], n1 * W)
+    products(T.ps1, road[1][2], "m1%d", not keeps)
+    if not keeps:
+        evac(T.ps1, n1, "m1%d", 1, lambda i: T.hB[:, i:4 * n1:4], S.ev1, "vsvs")
+        pack("hB", n1, S.ev1, 4, S.hqB)
+        leave(road[1], "hB")
 
     g.tensor.wait_ge(S.ev0, 4)
     products(T.ps0, [partner], "m0%d", True)
     evac(T.ps0, W, "m0%d", 2, lambda i: T.hP[:, i:TW:4], S.ev0, "vsvs")
     pack("hP", W, S.ev0, 8, S.hqP)
-    g.wait_ge(S.hqP, 1)
-    send(cores[partner], "hP", "lP", S.pa, W)
+    send(cores[partner], "hP", "lP", S.pa, S.pa, W)
 
-    if kept is not None:
-        sum_stage(False)
+    g.tensor.wait_ge(S.sel, 4)
+    if keeps:
+        g.tensor.wait_ge(S.sq, len(bits(cores[partner], core)))
+        g.tensor.wait_ge(S.ss, len(bits(cores[partner], core)))
+        unpack(T.ps1, n1, "lS", True, "m1%d")
+        evac(T.ps1, n1, "m1%d", 1, lambda i: T.hB[:, i:4 * n1:4], S.ev1, "vsvs")
+        pack("hB", n1, S.ev1, 4, S.hqB)
+        scatter("hB", road[1][2], "q")
+        scatter("hB", road[1][2], "s")
 
     g.tensor.wait_ge(S.ev0, 8)
     products(T.ps0, [rank], "m0%d", False)
-    g.tensor.wait_ge(S.sel, 4)
-    srcs = sources(rank)
     arrivals = [("lP", S.pa, 2 * len(bits(cores[partner], core)))]
-    for k, j in enumerate(srcs):
-        arrivals.append(("lX%d" % k, S["x%d" % k], 2 * (len(bits(j[0], core)) // len(j[1]))))
+    for k, (c, nd) in enumerate(sources(rank)):
+        arrivals.append(("lX%d" % k, S["x%d" % k], 2 * (len(bits(c, core)) // nd)))
     for k, (land, sem, cnt) in enumerate(arrivals):
         g.tensor.wait_ge(sem, cnt)
-        last = k == len(arrivals) - 1
-        for i in range(4):
-            sq, ss = pick(i)
-            ins = g.tensor.matmul_mx(T.ps0[:, 512 * i:512 * i + W], sq, ss, T[land + "q"][:, 0:W], T[land + "s"][:, 0:W],
-                                     False, last)
-            if last:
-                ins.then_inc(S["m0%d" % i], 1)
+        unpack(T.ps0, W, land, k == len(arrivals) - 1, "m0%d")
     evac(T.ps0, W, "m0%d", 3, lambda i: T.ysb[:, i:TW:4], S.yev, "vsvs")
     g.sync.wait_ge(S.yev, 4)
     g.sync.dma_start(T.y[:], T.ysb[:]).then_inc(S.st, 16)

@@ -27,8 +27,8 @@ SCRATCH = {
     "ps0": ("psum", [128, 4 * 512], "float32"),
     "ps1": ("psum", [128, 4 * 512], "float32"),
 }
-SEMAPHORES = (["c1", "c2", "sel", "ev0", "ev1", "hqA", "hqB", "hqP", "sq", "ss", "pa", "x0", "x1", "x2", "sent", "yev",
-               "st"]
+SEMAPHORES = (["c1", "c2", "sel", "ev0", "ev1", "hqA", "hqB0", "hqB1", "hqP", "sq", "ss", "pa", "x0", "x1", "x2", "sent",
+               "yev", "st"]
               + ["ld%d" % k for k in range(10)] + ["aq%d" % i for i in range(4)] + ["bq%d" % k for k in range(6)]
               + ["m0%d" % i for i in range(4)] + ["m1%d" % i for i in range(4)])
 
@@ -122,15 +122,22 @@ def rank_program(g, core, T, topo):
             return ("keep", 3) if road[1] == c else ("feed", 0)
         return ("direct", 1) if all(topo.may_write(c, cores[d]) for d in road[2]) else ("feed", 2)
 
+    def work_of(c):
+        return sorted(plan[topo.chip(c)], key=lambda j: part_of(c, j)[1])
+
     def sources(d):
         out = []
         for Y in plan:
             for road in plan[Y]:
-                if d in road[2]:
-                    out.append((1 if road[0] == "sum" else 2, road[1], len(road[2])))
-                    if road[0] == "relay":
-                        out += [(0, c, len(road[2])) for c in cores
-                                if topo.chip(c) == Y and part_of(c, road)[0] == "direct"]
+                if d not in road[2]:
+                    continue
+                if road[0] == "sum":
+                    out.append((2, road[1], 1))
+                    continue
+                there = [c for c in cores if topo.chip(c) == Y]
+                feeder = [c for c in there if part_of(c, road)[0] == "feed"][0]
+                out.append((1 if work_of(feeder)[0] == road else 3, road[1], len(road[2])))
+                out += [(0, c, len(road[2])) for c in there if part_of(c, road)[0] == "direct"]
         return [(s[1], s[2]) for s in sorted(out, key=lambda s: s[0])]
 
     def send(dst, name, land, semq, sems, ncol):
@@ -139,6 +146,16 @@ def rank_program(g, core, T, topo):
         g.remote_dma(T[land + "q"][:, 0:ncol].bitcast(u8), T[name + "q"][:, 0:ncol].bitcast(u8), semq, S.sent,
                      pid, rid, to_mask(es))
         g.remote_dma(T[land + "s"][:, 0:ncol], T[name + "s"][:, 0:ncol], sems, S.sent, pid, rid, to_mask(es))
+        sent[0] += 2 * len(es)
+
+    def send_sum(name, k, d):
+        rid, pid, _se = topo.addr(cores[d])
+        es = bits(core, cores[d])
+        slot = [s[0] for s in sources(d)].index(core)
+        g.remote_dma(T["lX%dq" % slot][:, 0:W].bitcast(u8), T[name + "q"][:, W * k:W * k + W].bitcast(u8),
+                     S["x%d" % slot], S.sent, pid, rid, to_mask(es))
+        g.remote_dma(T["lX%ds" % slot][:, 0:W], T[name + "s"][:, W * k:W * k + W], S["x%d" % slot], S.sent,
+                     pid, rid, to_mask(es))
         sent[0] += 2 * len(es)
 
     def scatter(name, dests, part):
@@ -165,23 +182,51 @@ def rank_program(g, core, T, topo):
         g.wait_ge(S.sent, sent[0])
         return
 
-    def evac(ps, ncol, mm, cnt, out_of, done, who):
-        for i in range(4):
-            src = ps[:, 512 * i:512 * i + ncol]
-            if who[i] == "v":
-                g.vector.wait_ge(S[mm % i], cnt)
-                g.vector.tensor_copy(out_of(i), src).then_inc(done, 1)
-            else:
-                g.scalar.wait_ge(S[mm % i], cnt)
-                g.scalar.activation(out_of(i), src, ActivationFunctionType.Copy).then_inc(done, 1)
+    P = [T.ps0, T.ps1]
+    mc, ec = {}, [0, 0]
 
-    def pack(name, ncol, ev, cnt, done):
-        g.vector.wait_ge(ev, cnt)
-        g.vector.quantize_mx(T[name + "q"][:, 0:ncol], T[name + "s"][:, 0:ncol], T[name][:, 0:4 * ncol]).then_inc(done, 1)
-        g.wait_ge(done, 1)
+    def mm(s, i, lq, ls, rq, rs, start, stop):
+        ins = g.tensor.matmul_mx(P[s][:, 512 * i:512 * i + W], lq, ls, rq, rs, start, stop)
+        if stop:
+            ins.then_inc(S["m%d%d" % (s, i)], 1)
+            mc[(s, i)] = mc.get((s, i), 0) + 1
+
+    def prod(s, i, t, stop):
+        mm(s, i, T.aq[:, W * i:W * i + W], T.asc[:, W * i:W * i + W], T.bq[:, W * t:W * t + W],
+           T.bsc[:, W * t:W * t + W], True, stop)
+
+    def free(s, t):
+        if ec[s]:
+            g.tensor.wait_ge(S["ev%d" % s], ec[s])
+        g.tensor.wait_ge(S["bq%d" % t], 1)
+
+    def out(s, i, dst, who, done=None):
+        src = P[s][:, 512 * i:512 * i + W]
+        if done is None:
+            done = S["ev%d" % s]
+            ec[s] += 1
+        if who == "v":
+            g.vector.wait_ge(S["m%d%d" % (s, i)], mc[(s, i)])
+            g.vector.tensor_copy(dst, src).then_inc(done, 1)
+        else:
+            g.scalar.wait_ge(S["m%d%d" % (s, i)], mc[(s, i)])
+            g.scalar.activation(dst, src, ActivationFunctionType.Copy).then_inc(done, 1)
+
+    def slot_of(name, k, i):
+        return T[name][:, TW * k + i:TW * k + TW:4]
+
+    def pack(name, k, s, done):
+        g.vector.wait_ge(S["ev%d" % s], ec[s])
+        g.vector.quantize_mx(T[name + "q"][:, W * k:W * k + W], T[name + "s"][:, W * k:W * k + W],
+                             T[name][:, TW * k:TW * k + TW]).then_inc(done, 1)
 
     def pick(i):
         return T.sq[:, W * i:W * i + W], T.ssc[:, W * i:W * i + W]
+
+    def unpack(s, land, k, last):
+        for i in range(4):
+            sq, ss = pick(i)
+            mm(s, i, sq, ss, T[land + "q"][:, W * k:W * k + W], T[land + "s"][:, W * k:W * k + W], False, last)
 
     def leave(road, name):
         if part_of(core, road)[0] == "feed":
@@ -191,10 +236,10 @@ def rank_program(g, core, T, topo):
             scatter(name, road[2], "s")
 
     partner = [r for r in mine if r != rank][0]
-    road = sorted(plan[X], key=lambda j: part_of(core, j)[1])
+    road = work_of(core)
     keeps = part_of(core, road[1])[0] == "keep"
-    order = road[0][2] + road[1][2] + [partner, rank]
-    pos = {t: k for k, t in enumerate(order)}
+    rest = ([partner] + road[1][2] + [rank]) if keeps else (road[1][2] + [partner, rank])
+    pos = {t: k for k, t in enumerate(rest)}
     loads, ld_b, ld_a = [], {}, {}
     for r in _runs(road[0][2]):
         for t in r:
@@ -205,7 +250,7 @@ def rank_program(g, core, T, topo):
         for i in range(per * h, per * h + per):
             ld_a[i] = len(loads)
         loads.append((T.a_sb, T.a, TW * per * h, TW * per * (h + 1)))
-    for r in sorted(_runs([t for t in order if t not in road[0][2]]), key=lambda r: min(pos[t] for t in r)):
+    for r in sorted(_runs(rest), key=lambda r: min(pos[t] for t in r)):
         for t in r:
             ld_b[t] = len(loads)
         loads.append((T.b_sb, T.b, TW * r[0], TW * (r[-1] + 1)))
@@ -213,39 +258,17 @@ def rank_program(g, core, T, topo):
         q = g.sync if k % 2 == 0 else g.scalar
         q.dma_start(buf[:, c0:c1], src[:, c0:c1]).then_inc(S["ld%d" % k], 16)
 
+    def when(t):
+        return (ld_b[t], pos[t])
+
+    def quant_b(t):
+        g.vector.wait_ge(S["ld%d" % ld_b[t]], 16)
+        g.vector.quantize_mx(T.bq[:, W * t:W * t + W], T.bsc[:, W * t:W * t + W],
+                             T.b_sb[:, TW * t:TW * t + TW]).then_inc(S["bq%d" % t], 1)
+
     g.vector.memset(T.e_sb[:], 1.0).then_inc(S.c1, 1)
     g.wait_ge(S.c1, 1)
     g.affine_select(T.e_sb[:], T.e_sb[:], [[-1, EW]], AluOpType.is_equal, 0.0, 3, 4).then_inc(S.c2, 1)
-    g.vector.wait_ge(S.c2, 1)
-    for i in range(4):
-        sq, ss = pick(i)
-        g.vector.quantize_mx(sq, ss, T.e_sb[:, 3 - i:3 - i + TW]).then_inc(S.sel, 1)
-
-    def quant_b(t):
-        k = pos[t]
-        g.vector.wait_ge(S["ld%d" % ld_b[t]], 16)
-        g.vector.quantize_mx(T.bq[:, W * k:W * k + W], T.bsc[:, W * k:W * k + W],
-                             T.b_sb[:, TW * t:TW * t + TW]).then_inc(S["bq%d" % k], 1)
-
-    def products(ps, tiles, mm, stop, first=False):
-        k0, nc = pos[tiles[0]], W * len(tiles)
-        for t in tiles:
-            g.tensor.wait_ge(S["bq%d" % pos[t]], 1)
-        for i in range(4):
-            if first:
-                g.tensor.wait_ge(S["aq%d" % i], 1)
-            ins = g.tensor.matmul_mx(ps[:, 512 * i:512 * i + nc], T.aq[:, W * i:W * i + W], T.asc[:, W * i:W * i + W],
-                                     T.bq[:, W * k0:W * k0 + nc], T.bsc[:, W * k0:W * k0 + nc], True, stop)
-            if stop:
-                ins.then_inc(S[mm % i], 1)
-
-    def unpack(ps, nc, land, last, mm):
-        for i in range(4):
-            sq, ss = pick(i)
-            ins = g.tensor.matmul_mx(ps[:, 512 * i:512 * i + nc], sq, ss, T[land + "q"][:, 0:nc], T[land + "s"][:, 0:nc],
-                                     False, last)
-            if last:
-                ins.then_inc(S[mm % i], 1)
 
     for t in road[0][2]:
         quant_b(t)
@@ -253,46 +276,88 @@ def rank_program(g, core, T, topo):
         g.vector.wait_ge(S["ld%d" % ld_a[i]], 16)
         g.vector.quantize_mx(T.aq[:, W * i:W * i + W], T.asc[:, W * i:W * i + W],
                              T.a_sb[:, TW * i:TW * i + TW]).then_inc(S["aq%d" % i], 1)
-    n0, n1 = W * len(road[0][2]), W * len(road[1][2])
-    products(T.ps0, road[0][2], "m0%d", True, first=True)
-    evac(T.ps0, n0, "m0%d", 1, lambda i: T.hA[:, i:4 * n0:4], S.ev0, "sssv")
-    pack("hA", n0, S.ev0, 4, S.hqA)
+        if i % per == per - 1:
+            g.vector.wait_ge(S.c2, 1)
+            for j in range(i - per + 1, i + 1):
+                sq, ss = pick(j)
+                g.vector.quantize_mx(sq, ss, T.e_sb[:, 3 - j:3 - j + TW]).then_inc(S.sel, 1)
+    for k, t in enumerate(road[0][2]):
+        free(k, t)
+    for i in range(4):
+        g.tensor.wait_ge(S["aq%d" % i], 1)
+        for k, t in enumerate(road[0][2]):
+            prod(k, i, t, True)
+    for i in range(4):
+        out(0, i, slot_of("hA", 0, i), "s" if i < 3 else "v")
+        out(1, i, slot_of("hA", 1, i), "s")
+    pack("hA", 0, 0, S.hqA)
+    pack("hA", 1, 1, S.hqA)
+    g.wait_ge(S.hqA, 2)
     leave(road[0], "hA")
 
-    for t in sorted([t for t in order if t not in road[0][2]], key=lambda t: (ld_b[t], pos[t])):
-        quant_b(t)
-
-    products(T.ps1, road[1][2], "m1%d", not keeps)
-    if not keeps:
-        evac(T.ps1, n1, "m1%d", 1, lambda i: T.hB[:, i:4 * n1:4], S.ev1, "vsvs")
-        pack("hB", n1, S.ev1, 4, S.hqB)
-        leave(road[1], "hB")
-
-    g.tensor.wait_ge(S.ev0, 4)
-    products(T.ps0, [partner], "m0%d", True)
-    evac(T.ps0, W, "m0%d", 2, lambda i: T.hP[:, i:TW:4], S.ev0, "vsvs")
-    pack("hP", W, S.ev0, 8, S.hqP)
-    send(cores[partner], "hP", "lP", S.pa, S.pa, W)
-
-    g.tensor.wait_ge(S.sel, 4)
+    ks = sorted(range(len(road[1][2])), key=lambda k: when(road[1][2][k]))
     if keeps:
+        for t in sorted(rest, key=when):
+            quant_b(t)
+        free(0, partner)
+        for i in range(4):
+            prod(0, i, partner, True)
+        for i in range(4):
+            out(0, i, slot_of("hP", 0, i), "s")
+        pack("hP", 0, 0, S.hqP)
+        g.wait_ge(S.hqP, 1)
+        send(cores[partner], "hP", "lP", S.pa, S.pa, W)
+        sets = (1, 0)
+        for s, k in zip(sets, ks):
+            free(s, road[1][2][k])
+            for i in range(4):
+                prod(s, i, road[1][2][k], False)
+        g.tensor.wait_ge(S.sel, 4)
         g.tensor.wait_ge(S.sq, len(bits(cores[partner], core)))
         g.tensor.wait_ge(S.ss, len(bits(cores[partner], core)))
-        unpack(T.ps1, n1, "lS", True, "m1%d")
-        evac(T.ps1, n1, "m1%d", 1, lambda i: T.hB[:, i:4 * n1:4], S.ev1, "vsvs")
-        pack("hB", n1, S.ev1, 4, S.hqB)
-        scatter("hB", road[1][2], "q")
-        scatter("hB", road[1][2], "s")
+        for n, (s, k) in enumerate(zip(sets, ks)):
+            unpack(s, "lS", k, True)
+            for i in range(4):
+                out(s, i, slot_of("hB", k, i), ("vsvs", "svsv")[n][i])
+            pack("hB", k, s, S["hqB%d" % n])
+            g.wait_ge(S["hqB%d" % n], 1)
+            send_sum("hB", k, road[1][2][k])
+    else:
+        for k in ks:
+            quant_b(road[1][2][k])
+        for n, k in enumerate(ks):
+            free(n, road[1][2][k])
+            for i in range(4):
+                prod(n, i, road[1][2][k], True)
+            for i in range(4):
+                out(n, i, slot_of("hB", k, i), "svsv"[i])
+            pack("hB", k, n, S["hqB%d" % n])
+        g.wait_ge(S.hqB0, 1)
+        g.wait_ge(S.hqB1, 1)
+        leave(road[1], "hB")
+        quant_b(partner)
+        quant_b(rank)
+        free(0, partner)
+        for i in range(4):
+            prod(0, i, partner, True)
+        for i in range(4):
+            out(0, i, slot_of("hP", 0, i), "svsv"[i])
+        pack("hP", 0, 0, S.hqP)
+        g.wait_ge(S.hqP, 1)
+        send(cores[partner], "hP", "lP", S.pa, S.pa, W)
+        g.tensor.wait_ge(S.sel, 4)
 
-    g.tensor.wait_ge(S.ev0, 8)
-    products(T.ps0, [rank], "m0%d", False)
+    free(1, rank)
+    for i in range(4):
+        prod(1, i, rank, False)
     arrivals = [("lP", S.pa, 2 * len(bits(cores[partner], core)))]
     for k, (c, nd) in enumerate(sources(rank)):
         arrivals.append(("lX%d" % k, S["x%d" % k], 2 * (len(bits(c, core)) // nd)))
     for k, (land, sem, cnt) in enumerate(arrivals):
         g.tensor.wait_ge(sem, cnt)
-        unpack(T.ps0, W, land, k == len(arrivals) - 1, "m0%d")
-    evac(T.ps0, W, "m0%d", 3, lambda i: T.ysb[:, i:TW:4], S.yev, "vsvs")
+        unpack(1, land, 0, k == len(arrivals) - 1)
+    for i in range(4):
+        out(1, i, T.ysb[:, i:TW:4], "vsvs"[i], S.yev)
     g.sync.wait_ge(S.yev, 4)
     g.sync.dma_start(T.y[:], T.ysb[:]).then_inc(S.st, 16)
     g.sync.wait_ge(S.st, 16)

from concourse.bass import DstId, RemoteDMATransfer
from concourse.mybir import dt, AluOpType, ActivationFunctionType

W = 128
TW = 4 * W
NSIM = 128
EW = TW + 4
A_PARTS = 2
X4 = "float8_e4m3fn_x4"

SCRATCH = {
    "a_sb": ("sbuf", [128, 4 * TW], "bfloat16"),
    "b_sb": ("sbuf", [128, 6 * TW], "bfloat16"),
    "aq": ("sbuf", [128, 4 * W], X4), "asc": ("sbuf", [128, 4 * W], "uint8"),
    "bq": ("sbuf", [128, 6 * W], X4), "bsc": ("sbuf", [128, 6 * W], "uint8"),
    "e_sb": ("sbuf", [128, EW], "bfloat16"),
    "sq": ("sbuf", [128, 4 * W], X4), "ssc": ("sbuf", [128, 4 * W], "uint8"),
    "hA": ("sbuf", [128, 2 * TW], "bfloat16"), "hAq": ("sbuf", [128, 2 * W], X4), "hAs": ("sbuf", [128, 2 * W], "uint8"),
    "hB": ("sbuf", [128, 2 * TW], "bfloat16"), "hBq": ("sbuf", [128, 2 * W], X4), "hBs": ("sbuf", [128, 2 * W], "uint8"),
    "hP": ("sbuf", [128, TW], "bfloat16"), "hPq": ("sbuf", [128, W], X4), "hPs": ("sbuf", [128, W], "uint8"),
    "lSq": ("sbuf", [128, 2 * W], X4), "lSs": ("sbuf", [128, 2 * W], "uint8"),
    "lPq": ("sbuf", [128, W], X4), "lPs": ("sbuf", [128, W], "uint8"),
    "lX0q": ("sbuf", [128, W], X4), "lX0s": ("sbuf", [128, W], "uint8"),
    "lX1q": ("sbuf", [128, W], X4), "lX1s": ("sbuf", [128, W], "uint8"),
    "lX2q": ("sbuf", [128, W], X4), "lX2s": ("sbuf", [128, W], "uint8"),
    "ysb": ("sbuf", [128, TW], "float32"),
    "ps0": ("psum", [128, 4 * 512], "float32"),
    "ps1": ("psum", [128, 4 * 512], "float32"),
}
SEMAPHORES = (["c1", "c2", "sel", "ev0", "ev1", "hqA", "hqB0", "hqB1", "hqP", "sq", "ss", "pa", "x0", "x1", "x2", "sent",
               "yev", "st"]
              + ["ld%d" % k for k in range(10)] + ["aq%d" % i for i in range(4)] + ["bq%d" % k for k in range(6)]
              + ["m0%d" % i for i in range(4)] + ["m1%d" % i for i in range(4)])


def _outside(cores, topo, X, dests, dies):
    for c in range(NSIM):
        if (topo.chip(c) == X and c not in cores and topo.die(c) not in dies
                and all(topo.may_write(c, cores[r]) for r in dests)):
            return c
    return None


def _plan(cores, topo):
    plan = {}
    for c0 in cores:
        X = topo.chip(c0)
        if X in plan:
            continue
        mine = [c for c in cores if topo.chip(c) == X]
        off = [r for r in range(len(cores)) if topo.chip(cores[r]) != X]
        share = len(off) // 2
        left, roads, able = list(off), [], []
        for c in mine:
            can = [r for r in off if topo.may_write(c, cores[r])]
            if len(can) == len(off):
                able.append(c)
            elif len(can) >= share:
                take = [r for r in can if r in left][:share]
                roads.append(("sum", c, take))
                left = [r for r in left if r not in take]
        need = len(left) // share
        heads = able[:need]
        if len(heads) < need:
            heads.append(_outside(cores, topo, X, left, [topo.die(s) for s in heads]))
        if need == 1:
            roads.append(("sum", heads[0], left))
        elif need == 2:
            near = [r for r in left if topo.die(cores[r]) == topo.die(heads[0])]
            if len(near) != share:
                near = left[:share]
            for s, ds in ((heads[0], near), (heads[1], [r for r in left if r not in near])):
                roads.append(("sum" if s in cores else "relay", s, ds))
        plan[X] = roads
    for Z in plan:
        dies = []
        for X in plan:
            for k, road in enumerate(plan[X]):
                if road[0] == "sum" and all(topo.chip(cores[d]) == Z for d in road[2]):
                    if topo.die(road[1]) in dies:
                        h = _outside(cores, topo, X, road[2], dies)
                        if h is not None:
                            plan[X][k] = ("relay", h, road[2])
                    dies.append(topo.die(plan[X][k][1]))
    return plan


def _runs(ts):
    out = []
    for t in sorted(ts):
        if out and out[-1][-1] == t - 1:
            out[-1].append(t)
        else:
            out.append([t])
    return out


def rank_program(g, core, T, topo):
    cores = [int(c) for c in T.cores]
    plan = _plan(cores, topo)
    X = topo.chip(core)
    if X not in plan:
        return
    rank = T.rank_of(core)
    headed = ([j for j in plan[X] if j[1] == core] + [None])[0]
    if rank is None and headed is None:
        return
    S = T.sem
    u8 = dt.uint8
    mine = [r for r in range(len(cores)) if topo.chip(cores[r]) == X]
    sent = [0]

    def bits(src, dst):
        m = topo.mask(src, dst)
        return [e for e in range(m.bit_length()) if (m >> e) & 1]

    def to_mask(es):
        return sum(1 << e for e in es)

    def part_of(c, road):
        if road[0] == "sum":
            return ("keep", 3) if road[1] == c else ("feed", 0)
        return ("direct", 1) if all(topo.may_write(c, cores[d]) for d in road[2]) else ("feed", 2)

    def work_of(c):
        return sorted(plan[topo.chip(c)], key=lambda j: part_of(c, j)[1])

    def sources(d):
        out = []
        for Y in plan:
            for road in plan[Y]:
                if d not in road[2]:
                    continue
                if road[0] == "sum":
                    out.append((2, road[1], 1))
                    continue
                there = [c for c in cores if topo.chip(c) == Y]
                feeder = [c for c in there if part_of(c, road)[0] == "feed"][0]
                out.append((1 if work_of(feeder)[0] == road else 3, road[1], len(road[2])))
                out += [(0, c, len(road[2])) for c in there if part_of(c, road)[0] == "direct"]
        return [(s[1], s[2]) for s in sorted(out, key=lambda s: s[0])]

    def send(dst, name, land, semq, sems, ncol):
        rid, pid, _se = topo.addr(dst)
        es = bits(core, dst)
        g.remote_dma(T[land + "q"][:, 0:ncol].bitcast(u8), T[name + "q"][:, 0:ncol].bitcast(u8), semq, S.sent,
                     pid, rid, to_mask(es))
        g.remote_dma(T[land + "s"][:, 0:ncol], T[name + "s"][:, 0:ncol], sems, S.sent, pid, rid, to_mask(es))
        sent[0] += 2 * len(es)

    def send_sum(name, k, d):
        rid, pid, _se = topo.addr(cores[d])
        es = bits(core, cores[d])
        slot = [s[0] for s in sources(d)].index(core)
        g.remote_dma(T["lX%dq" % slot][:, 0:W].bitcast(u8), T[name + "q"][:, W * k:W * k + W].bitcast(u8),
                     S["x%d" % slot], S.sent, pid, rid, to_mask(es))
        g.remote_dma(T["lX%ds" % slot][:, 0:W], T[name + "s"][:, W * k:W * k + W], S["x%d" % slot], S.sent,
                     pid, rid, to_mask(es))
        sent[0] += 2 * len(es)

    def scatter(name, dests, part):
        nd, trs = len(dests), []
        for k, d in enumerate(dests):
            rid, pid, _se = topo.addr(cores[d])
            es = bits(core, cores[d])
            es = es[k * (len(es) // nd):(k + 1) * (len(es) // nd)]
            slot = [s[0] for s in sources(d)].index(core)
            src, dst = T[name + part][:, W * k:W * k + W], T["lX%d%s" % (slot, part)][:, 0:W]
            if part == "q":
                src, dst = src.bitcast(u8), dst.bitcast(u8)
            trs.append(RemoteDMATransfer(dst_ids=[DstId(rid=rid, pnc=pid)], dma_engine_mask=to_mask(es),
                                         remote_sem=S["x%d" % slot], src=src, dst=dst))
            sent[0] += len(es)
        g.remote_dma_fused(trs, local_sem=S.sent)

    if rank is None:
        feeder = [cores[r] for r in mine if part_of(cores[r], headed)[0] == "feed"][0]
        g.wait_ge(S.sq, len(bits(feeder, core)))
        scatter("lS", headed[2], "q")
        g.wait_ge(S.ss, len(bits(feeder, core)))
        scatter("lS", headed[2], "s")
        g.wait_ge(S.sent, sent[0])
        return

    P = [T.ps0, T.ps1]
    mc, ec = {}, [0, 0]

    def mm(s, i, lq, ls, rq, rs, start, stop):
        ins = g.tensor.matmul_mx(P[s][:, 512 * i:512 * i + W], lq, ls, rq, rs, start, stop)
        if stop:
            ins.then_inc(S["m%d%d" % (s, i)], 1)
            mc[(s, i)] = mc.get((s, i), 0) + 1

    def prod(s, i, t, stop):
        mm(s, i, T.aq[:, W * i:W * i + W], T.asc[:, W * i:W * i + W], T.bq[:, W * t:W * t + W],
           T.bsc[:, W * t:W * t + W], True, stop)

    def free(s, t):
        if ec[s]:
            g.tensor.wait_ge(S["ev%d" % s], ec[s])
        g.tensor.wait_ge(S["bq%d" % t], 1)

    def out(s, i, dst, who, done=None):
        src = P[s][:, 512 * i:512 * i + W]
        if done is None:
            done = S["ev%d" % s]
            ec[s] += 1
        if who == "v":
            g.vector.wait_ge(S["m%d%d" % (s, i)], mc[(s, i)])
            g.vector.tensor_copy(dst, src).then_inc(done, 1)
        else:
            g.scalar.wait_ge(S["m%d%d" % (s, i)], mc[(s, i)])
            g.scalar.activation(dst, src, ActivationFunctionType.Copy).then_inc(done, 1)

    def slot_of(name, k, i):
        return T[name][:, TW * k + i:TW * k + TW:4]

    def pack(name, k, s, done):
        g.vector.wait_ge(S["ev%d" % s], ec[s])
        g.vector.quantize_mx(T[name + "q"][:, W * k:W * k + W], T[name + "s"][:, W * k:W * k + W],
                             T[name][:, TW * k:TW * k + TW]).then_inc(done, 1)

    def pick(i):
        return T.sq[:, W * i:W * i + W], T.ssc[:, W * i:W * i + W]

    def unpack(s, land, k, last):
        for i in range(4):
            sq, ss = pick(i)
            mm(s, i, sq, ss, T[land + "q"][:, W * k:W * k + W], T[land + "s"][:, W * k:W * k + W], False, last)

    def leave(road, name):
        if part_of(core, road)[0] == "feed":
            send(road[1], name, "lS", S.sq, S.ss, W * len(road[2]))
        else:
            scatter(name, road[2], "q")
            scatter(name, road[2], "s")

    partner = [r for r in mine if r != rank][0]
    road = work_of(core)
    keeps = part_of(core, road[1])[0] == "keep"
    rest = ([partner] + road[1][2] + [rank]) if keeps else (road[1][2] + [partner, rank])
    pos = {t: k for k, t in enumerate(rest)}
    loads, ld_b, ld_a = [], {}, {}
    for r in _runs(road[0][2]):
        for t in r:
            ld_b[t] = len(loads)
        loads.append((T.b_sb, T.b, TW * r[0], TW * (r[-1] + 1)))
    per = 4 // A_PARTS
    for h in range(A_PARTS):
        for i in range(per * h, per * h + per):
            ld_a[i] = len(loads)
        loads.append((T.a_sb, T.a, TW * per * h, TW * per * (h + 1)))
    for r in sorted(_runs(rest), key=lambda r: min(pos[t] for t in r)):
        for t in r:
            ld_b[t] = len(loads)
        loads.append((T.b_sb, T.b, TW * r[0], TW * (r[-1] + 1)))
    for k, (buf, src, c0, c1) in enumerate(loads):
        q = g.sync if k % 2 == 0 else g.scalar
        q.dma_start(buf[:, c0:c1], src[:, c0:c1]).then_inc(S["ld%d" % k], 16)

    def when(t):
        return (ld_b[t], pos[t])

    def quant_b(t):
        g.vector.wait_ge(S["ld%d" % ld_b[t]], 16)
        g.vector.quantize_mx(T.bq[:, W * t:W * t + W], T.bsc[:, W * t:W * t + W],
                             T.b_sb[:, TW * t:TW * t + TW]).then_inc(S["bq%d" % t], 1)

    g.vector.memset(T.e_sb[:], 1.0).then_inc(S.c1, 1)
    g.wait_ge(S.c1, 1)
    g.affine_select(T.e_sb[:], T.e_sb[:], [[-1, EW]], AluOpType.is_equal, 0.0, 3, 4).then_inc(S.c2, 1)

    for t in road[0][2]:
        quant_b(t)
    for i in range(4):
        g.vector.wait_ge(S["ld%d" % ld_a[i]], 16)
        g.vector.quantize_mx(T.aq[:, W * i:W * i + W], T.asc[:, W * i:W * i + W],
                             T.a_sb[:, TW * i:TW * i + TW]).then_inc(S["aq%d" % i], 1)
        if i % per == per - 1:
            g.vector.wait_ge(S.c2, 1)
            for j in range(i - per + 1, i + 1):
                sq, ss = pick(j)
                g.vector.quantize_mx(sq, ss, T.e_sb[:, 3 - j:3 - j + TW]).then_inc(S.sel, 1)
    for k, t in enumerate(road[0][2]):
        free(k, t)
    for i in range(4):
        g.tensor.wait_ge(S["aq%d" % i], 1)
        for k, t in enumerate(road[0][2]):
            prod(k, i, t, True)
    for i in range(4):
        out(0, i, slot_of("hA", 0, i), "s" if i < 3 else "v")
        out(1, i, slot_of("hA", 1, i), "s")
    pack("hA", 0, 0, S.hqA)
    pack("hA", 1, 1, S.hqA)
    g.wait_ge(S.hqA, 2)
    leave(road[0], "hA")

    ks = sorted(range(len(road[1][2])), key=lambda k: when(road[1][2][k]))
    if keeps:
        for t in sorted(rest, key=when):
            quant_b(t)
        free(0, partner)
        for i in range(4):
            prod(0, i, partner, True)
        for i in range(4):
            out(0, i, slot_of("hP", 0, i), "s")
        pack("hP", 0, 0, S.hqP)
        g.wait_ge(S.hqP, 1)
        send(cores[partner], "hP", "lP", S.pa, S.pa, W)
        sets = (1, 0)
        for s, k in zip(sets, ks):
            free(s, road[1][2][k])
            for i in range(4):
                prod(s, i, road[1][2][k], False)
        g.tensor.wait_ge(S.sel, 4)
        g.tensor.wait_ge(S.sq, len(bits(cores[partner], core)))
        g.tensor.wait_ge(S.ss, len(bits(cores[partner], core)))
        for n, (s, k) in enumerate(zip(sets, ks)):
            unpack(s, "lS", k, True)
            for i in range(4):
                out(s, i, slot_of("hB", k, i), ("vsvs", "svsv")[n][i])
            pack("hB", k, s, S["hqB%d" % n])
            g.wait_ge(S["hqB%d" % n], 1)
            send_sum("hB", k, road[1][2][k])
    else:
        for k in ks:
            quant_b(road[1][2][k])
        for n, k in enumerate(ks):
            free(n, road[1][2][k])
            for i in range(4):
                prod(n, i, road[1][2][k], True)
            for i in range(4):
                out(n, i, slot_of("hB", k, i), "svsv"[i])
            pack("hB", k, n, S["hqB%d" % n])
        g.wait_ge(S.hqB0, 1)
        g.wait_ge(S.hqB1, 1)
        leave(road[1], "hB")
        quant_b(partner)
        quant_b(rank)
        free(0, partner)
        for i in range(4):
            prod(0, i, partner, True)
        for i in range(4):
            out(0, i, slot_of("hP", 0, i), "svsv"[i])
        pack("hP", 0, 0, S.hqP)
        g.wait_ge(S.hqP, 1)
        send(cores[partner], "hP", "lP", S.pa, S.pa, W)
        g.tensor.wait_ge(S.sel, 4)

    free(1, rank)
    for i in range(4):
        prod(1, i, rank, False)
    arrivals = [("lP", S.pa, 2 * len(bits(cores[partner], core)))]
    for k, (c, nd) in enumerate(sources(rank)):
        arrivals.append(("lX%d" % k, S["x%d" % k], 2 * (len(bits(c, core)) // nd)))
    for k, (land, sem, cnt) in enumerate(arrivals):
        g.tensor.wait_ge(sem, cnt)
        unpack(1, land, 0, k == len(arrivals) - 1)
    for i in range(4):
        out(1, i, T.ysb[:, i:TW:4], "vsvs"[i], S.yev)
    g.sync.wait_ge(S.yev, 4)
    g.sync.dma_start(T.y[:], T.ysb[:]).then_inc(S.st, 16)
    g.sync.wait_ge(S.st, 16)
    g.wait_ge(S.sent, sent[0])
